import numpy as np
import ml_dtypes


def mxq(x, axis, fmt="e4m3"):
    dtype, down = {"e4m3": (ml_dtypes.float8_e4m3fn, 7), "e5m2": (ml_dtypes.float8_e5m2, 14)}[fmt]
    v = np.moveaxis(np.asarray(x, np.float32).astype(ml_dtypes.bfloat16).astype(np.float64), axis, -1)
    blocks = v.reshape(v.shape[:-1] + (-1, 32))
    amax = np.abs(blocks).max(-1, keepdims=True)
    byte = np.maximum(np.where(amax > 0, np.frexp(amax)[1] - 1 + 127, 0) - down, 1)
    scale = np.exp2(byte - 127.0)
    codes = (blocks / scale).astype(np.float32).astype(dtype).astype(np.float64)
    return np.moveaxis((codes * scale).reshape(v.shape), -1, axis)


WIDE = False


def mx_kscale(k):
    if not WIDE:
        return np.ones(k)
    levels = np.array([10, -10, 5, -5, 0])
    if k % 512:
        return np.exp2(np.random.permutation(np.resize(levels, k // 32))).repeat(32)
    a = np.empty((k // 512, 16))
    for p in range(k // 512):
        a[p, :8] = np.random.permutation(np.resize(levels, 8))
        for g in range(8):
            far = levels[np.abs(levels - a[p, g]) >= 10]
            a[p, g + 8] = far[np.random.randint(len(far))]
    return np.exp2(a.ravel()).repeat(32)


def f64(x):
    return np.asarray(x).astype(np.float64)


def striped(idx):
    return np.tile(idx.reshape(-1, 16).T, (8, 1)).astype(np.uint16)


def unstriped(offs):
    return offs[:16].T.reshape(-1).astype(np.int64)


def striped8(idx):
    return np.concatenate([x.reshape(-1, 16).T for x in idx]).astype(np.uint16)


def runs(offs, k):
    lists = np.stack([offs[16 * r : 16 * r + 16].T.reshape(-1) for r in range(8)]).astype(np.int64)
    return lists[np.arange(k) % 512 // 64]


def pack_weight(w):
    k, n = w.shape
    w = f64(np.asarray(w, np.float32).astype(ml_dtypes.bfloat16)).reshape(k // 32, 32, n)
    amax = np.abs(w).max(1)
    byte = np.clip(np.where(amax > 0, np.frexp(amax)[1] - 1 + 127 - 7, 1), 1, 254)
    scaled = (w * np.exp2(127.0 - byte)[:, None, :]).reshape(k, n).astype(np.float32)
    words = np.ascontiguousarray(scaled.reshape(k // 512, 128, 4, n).transpose(0, 1, 3, 2)).astype(ml_dtypes.float8_e4m3fn).view(np.uint8)
    return words, np.ascontiguousarray(byte.astype(np.uint8).reshape(k // 512, 16, n))


def unpack_weight(words, scales):
    g, p, n, _ = words.shape
    vals = np.ascontiguousarray(words).view(ml_dtypes.float8_e4m3fn).astype(np.float64) * np.repeat(np.exp2(scales.astype(np.float64) - 127.0), 8, axis=1)[..., None]
    return vals.transpose(0, 1, 3, 2).reshape(g * 512, n)


K, T, S, N, H = 512, 2048, 512, 512, 512


def setup_inputs():
    n = np.random.standard_normal
    s = mx_kscale(K)[:, None]
    u = mx_kscale(H)
    packed_xT = pack_weight(n((K, T)) * s)
    return {
        "x_words": packed_xT[0],
        "x_scales": packed_xT[1],
        "w1": (n((K, H)) / np.sqrt(K) / s).astype(np.float32),
        "gn": (np.random.uniform(0.5, 1.5, (H, 1)) * u[:, None]).astype(np.float32),
        "w2": (n((H, N)) / np.sqrt(H) / u[:, None]).astype(np.float32),
        "offs": striped(np.random.permutation(T)[:S]),
        "n1": striped8(np.stack([np.random.permutation(S) for _ in range(8)])),
        "n2": striped8(np.stack([np.random.permutation(S) for _ in range(8)])),
        "n3": striped8(np.stack([np.random.permutation(S) for _ in range(8)])),
    }


def reference(x_words, x_scales, w1, gn, w2, offs, n1, n2, n3):
    xq = unpack_weight(x_words, x_scales)[:, unstriped(offs)]
    y = mxq(f64(w1), 0, "e4m3").T @ xq
    z = f64(gn) * (y / (np.abs(y[np.arange(H)[:, None], runs(n1, H)]) + 0.5))
    h = mxq(f64(w2), 0, "e4m3").T @ mxq(z, 0, "e4m3")
    return 0.75 * (h * (y[np.arange(H)[:, None], runs(n3, H)]) - ((h[np.arange(N)[:, None], runs(n2, N)]) * y))

@@ -1,0 +1,132 @@
+from contextlib import ExitStack
+
+import concourse.mybir as mybir
+
+K, T, S, N, H = 512, 2048, 512, 512, 512
+FLOPS = 2 * K * H * S + 2 * H * N * S
+
+F32 = mybir.dt.float32
+BF16 = mybir.dt.bfloat16
+I32 = mybir.dt.int32
+U32 = mybir.dt.uint32
+U16 = mybir.dt.uint16
+U8 = mybir.dt.uint8
+FP8X4 = mybir.dt.float8_e4m3fn_x4
+ACT = mybir.ActivationFunctionType
+MULT = mybir.AluOpType.mult
+SUB = mybir.AluOpType.subtract
+
+P = 128
+PACK = 4
+
+
+def tile_picked_skipcrossbnorm_none_p_kernel(tc, x_words, x_scales, w1, gn, w2, offs, n1, n2, n3, out):
+    nc = tc.nc
+    with ExitStack() as ctx:
+        lists = ctx.enter_context(tc.tile_pool(name="lists", bufs=1))
+        keep = ctx.enter_context(tc.tile_pool(name="keep", bufs=1))
+        psum = ctx.enter_context(tc.psum_pool(name="psum", bufs=1))
+
+        offs_sb = lists.tile([P, S // 16], U16, name="offs_sb")
+        n1_sb = lists.tile([P, S // 16], U16, name="n1_sb")
+        n2_sb = lists.tile([P, S // 16], U16, name="n2_sb")
+        n3_sb = lists.tile([P, S // 16], U16, name="n3_sb")
+
+        xs_all = keep.tile([P, T], U8, name="xs_all", align_bytes=64)
+        xw_all = keep.tile([P, T], I32, name="xw_all", align_bytes=64)
+        w1_raw = keep.tile([P, PACK, H], F32, name="w1_raw", align_bytes=64)
+        w2_raw = keep.tile([P, PACK, N], F32, name="w2_raw", align_bytes=64)
+        gain = keep.tile([P, PACK], F32, name="gain")
+        four = keep.tile([P, 1], F32, name="four")
+        half = keep.tile([P, 1], F32, name="half")
+
+        nc.vector.memset(xs_all[:].bitcast(I32), 0)
+        nc.vector.memset(four[:], 4.0)
+        nc.scalar.activation(half[:], four[:], ACT.Abs_reciprocal_sqrt)
+
+        nc.sync.dma_start(w1_raw[:], w1.rearrange("(p j) c -> p j c", j=PACK))
+        nc.sync.dma_start(offs_sb[:], offs)
+        for q in range(4):
+            nc.scalar.dma_start(xs_all[32 * q : 32 * q + 4, :].bitcast(I32), x_scales[0, 4 * q : 4 * q + 4, :].bitcast(I32))
+        nc.sync.dma_start(xw_all[:], x_words[0].rearrange("p n t -> p (n t)").bitcast(I32))
+        nc.sync.dma_start(n1_sb[:], n1)
+        nc.sync.dma_start(gain[:], gn.rearrange("(p t) o -> p (t o)", t=PACK))
+        nc.sync.dma_start(w2_raw[:], w2.rearrange("(p j) c -> p j c", j=PACK))
+        nc.sync.dma_start(n3_sb[:], n3)
+        nc.sync.dma_start(n2_sb[:], n2)
+
+        def deal(engine_copy, grouped, raw, m0, m1):
+            engine_copy(
+                grouped[:].rearrange("p (t m j) -> p m t j", t=PACK, j=PACK)[:, m0:m1],
+                raw[:].rearrange("p j (m t) -> p m t j", t=PACK)[:, m0:m1],
+            )
+
+        xs = keep.tile([P, S], U8, name="xs", align_bytes=64)
+        xw = keep.tile([P, S], U32, name="xw", align_bytes=64)
+        w1_grouped = keep.tile([P, PACK * H], BF16, name="w1_grouped", align_bytes=64)
+        w1_codes = keep.tile([P, H], U32, name="w1_codes", align_bytes=64)
+        w1_scales = keep.tile([P, H], U8, name="w1_scales", align_bytes=64)
+        nc.vector.tensor_copy(xs[:], xs_all[:].indirect(offs_sb[:]))
+        deal(nc.scalar.copy, w1_grouped, w1_raw, 0, 64)
+        deal(nc.vector.tensor_copy, w1_grouped, w1_raw, 64, 128)
+        nc.vector.quantize_mx(out=w1_codes[:].bitcast(FP8X4), scales=w1_scales[:], in_=w1_grouped[:])
+        nc.vector.tensor_copy(xw[:], xw_all[:].bitcast(U32).indirect(offs_sb[:]))
+
+        y_ps = [psum.tile([P, S], F32, name=f"y_ps{t}") for t in range(PACK)]
+        h_ps = [psum.tile([P, S], F32, name=f"h_ps{t}") for t in range(PACK)]
+        y_win = [keep.tile([P, 2 * S], F32, name=f"y_win{t}", align_bytes=64) for t in range(PACK)]
+        r_win = [keep.tile([P, 2 * S], F32, name=f"r_win{t}", align_bytes=64) for t in range(PACK)]
+        h_win = [keep.tile([P, 2 * S], F32, name=f"h_win{t}", align_bytes=64) for t in range(PACK)]
+        z = keep.tile([P, PACK, S], F32, name="z", align_bytes=64)
+
+        for t in range(PACK):
+            cols = slice(t * P, (t + 1) * P)
+            nc.tensor.matmul_mx(out=y_ps[t][:], lhsT=w1_codes[:, cols].bitcast(FP8X4), lhsT_scale=w1_scales[:, cols],
+                                rhs=xw[:].bitcast(FP8X4), rhs_scale=xs[:], start=True, stop=True)
+
+        for t in range(PACK):
+            nc.scalar.activation(y_win[t][:, S:], y_ps[t][:], ACT.Abs)
+            nc.scalar.activation(r_win[t][:, S:], y_win[t][:, S:], ACT.Abs_reciprocal_sqrt, bias=half[:])
+            if t < 2:
+                nc.vector.tensor_copy(y_win[t][:, :S], y_ps[t][:])
+            else:
+                nc.scalar.copy(y_win[t][:, :S], y_ps[t][:])
+            nc.vector.scalar_tensor_tensor(r_win[t][:, :S], r_win[t][:, S:], gain[:, t : t + 1], r_win[t][:, S:], MULT, MULT)
+            nc.vector.tensor_tensor(z[:, t, :], r_win[t][:].indirect(n1_sb[:]), y_win[t][:, :S], MULT)
+
+        w2_grouped = keep.tile([P, PACK * N], BF16, name="w2_grouped", align_bytes=64)
+        w2_codes = keep.tile([P, N], U32, name="w2_codes", align_bytes=64)
+        w2_scales = keep.tile([P, N], U8, name="w2_scales", align_bytes=64)
+        for m0 in range(0, P, 32):
+            deal(nc.scalar.copy, w2_grouped, w2_raw, m0, m0 + 32)
+
+        z_grouped = keep.tile([P, PACK * S], BF16, name="z_grouped", align_bytes=64)
+        z_codes = keep.tile([P, S], U32, name="z_codes", align_bytes=64)
+        z_scales = keep.tile([P, S], U8, name="z_scales", align_bytes=64)
+        nc.vector.tensor_copy(
+            z_grouped[:].rearrange("p (c i t) -> p c t i", i=2, t=PACK),
+            z[:].rearrange("p t (c i) -> p c t i", i=2),
+        )
+        nc.vector.quantize_mx(out=w2_codes[:].bitcast(FP8X4), scales=w2_scales[:], in_=w2_grouped[:])
+        nc.vector.quantize_mx(out=z_codes[:].bitcast(FP8X4), scales=z_scales[:], in_=z_grouped[:])
+
+        for t in range(PACK):
+            cols = slice(t * P, (t + 1) * P)
+            nc.tensor.matmul_mx(out=h_ps[t][:], lhsT=w2_codes[:, cols].bitcast(FP8X4), lhsT_scale=w2_scales[:, cols],
+                                rhs=z_codes[:].bitcast(FP8X4), rhs_scale=z_scales[:], start=True, stop=True)
+
+        y3_first = keep.tile([P, S], F32, name="y3_first")
+        nc.vector.tensor_copy(y3_first[:], y_win[0][:].indirect(n3_sb[:]))
+
+        out_rows = out.rearrange("(p t) j -> p t j", t=PACK)
+        for t in range(PACK):
+            nc.scalar.activation(h_win[t][:, :S], h_ps[t][:], ACT.Copy, scale=0.75)
+            if t == 0:
+                nc.vector.tensor_tensor(h_win[t][:, S:], y3_first[:], h_win[t][:, :S], MULT)
+            else:
+                nc.vector.tensor_tensor(h_win[t][:, S:], y_win[t][:].indirect(n3_sb[:]), h_win[t][:, :S], MULT)
+            second = keep.tile([P, S], F32, name=f"second{t}")
+            nc.vector.tensor_tensor(second[:], h_win[t][:].indirect(n2_sb[:]), y_win[t][:, :S], MULT)
+            result = keep.tile([P, S], F32, name=f"result{t}")
+            nc.vector.tensor_tensor(result[:], h_win[t][:, S:], second[:], SUB)
+            nc.sync.dma_start(out_rows[:, t, :], result[:])

@@ -1,6 +1,7 @@
 from contextlib import ExitStack
 
 import concourse.mybir as mybir
+from concourse.masks import make_identity
 
 K, T, S, N, H = 512, 2048, 512, 512, 512
 FLOPS = 2 * K * H * S + 2 * H * N * S
@@ -14,6 +15,7 @@ U8 = mybir.dt.uint8
 FP8X4 = mybir.dt.float8_e4m3fn_x4
 ACT = mybir.ActivationFunctionType
 MULT = mybir.AluOpType.mult
+ADD = mybir.AluOpType.add
 SUB = mybir.AluOpType.subtract
 
 P = 128
@@ -32,28 +34,29 @@ def tile_picked_skipcrossbnorm_none_p_kernel(tc, x_words, x_scales, w1, gn, w2, 
         n2_sb = lists.tile([P, S // 16], U16, name="n2_sb")
         n3_sb = lists.tile([P, S // 16], U16, name="n3_sb")
 
-        xs_all = keep.tile([P, T], U8, name="xs_all", align_bytes=64)
+        xs_all = keep.tile([P, T], U8, tag="staged", name="xs_all", align_bytes=64)
         xw_all = keep.tile([P, T], I32, name="xw_all", align_bytes=64)
         w1_raw = keep.tile([P, PACK, H], F32, name="w1_raw", align_bytes=64)
-        w2_raw = keep.tile([P, PACK, N], F32, name="w2_raw", align_bytes=64)
         gain = keep.tile([P, PACK], F32, name="gain")
         four = keep.tile([P, 1], F32, name="four")
         half = keep.tile([P, 1], F32, name="half")
 
-        nc.vector.memset(xs_all[:].bitcast(I32), 0)
-        nc.vector.memset(four[:], 4.0)
-        nc.scalar.activation(half[:], four[:], ACT.Abs_reciprocal_sqrt)
-
-        nc.sync.dma_start(w1_raw[:], w1.rearrange("(p j) c -> p j c", j=PACK))
-        nc.sync.dma_start(offs_sb[:], offs)
+        nc.gpsimd.memset(xs_all[:].bitcast(I32), 0)
+        nc.gpsimd.memset(four[:], 4.0)
         for q in range(4):
             nc.scalar.dma_start(xs_all[32 * q : 32 * q + 4, :].bitcast(I32), x_scales[0, 4 * q : 4 * q + 4, :].bitcast(I32))
-        nc.sync.dma_start(xw_all[:], x_words[0].rearrange("p n t -> p (n t)").bitcast(I32))
+        nc.scalar.activation(half[:], four[:], ACT.Abs_reciprocal_sqrt)
+
+        nc.gpsimd.dma_start(gain[:], gn.rearrange("(p t) o -> p (t o)", t=PACK))
+        identity = keep.tile([P, P], F32, name="identity")
+        make_identity(nc, identity[:])
+
+        nc.sync.dma_start(offs_sb[:], offs)
         nc.sync.dma_start(n1_sb[:], n1)
-        nc.sync.dma_start(gain[:], gn.rearrange("(p t) o -> p (t o)", t=PACK))
-        nc.sync.dma_start(w2_raw[:], w2.rearrange("(p j) c -> p j c", j=PACK))
+        nc.sync.dma_start(w1_raw[:], w1.rearrange("(p j) c -> p j c", j=PACK))
         nc.sync.dma_start(n3_sb[:], n3)
         nc.sync.dma_start(n2_sb[:], n2)
+        nc.sync.dma_start(xw_all[:], x_words[0].rearrange("p n t -> p (n t)").bitcast(I32))
 
         def deal(engine_copy, grouped, raw, m0, m1):
             engine_copy(
@@ -70,63 +73,114 @@ def tile_picked_skipcrossbnorm_none_p_kernel(tc, x_words, x_scales, w1, gn, w2, 
         deal(nc.scalar.copy, w1_grouped, w1_raw, 0, 64)
         deal(nc.vector.tensor_copy, w1_grouped, w1_raw, 64, 128)
         nc.vector.quantize_mx(out=w1_codes[:].bitcast(FP8X4), scales=w1_scales[:], in_=w1_grouped[:])
-        nc.vector.tensor_copy(xw[:], xw_all[:].bitcast(U32).indirect(offs_sb[:]))
+        HALF = S // 2
+        for u in range(2):
+            nc.vector.tensor_copy(xw[:, u * HALF : (u + 1) * HALF], xw_all[:].bitcast(U32).indirect(offs_sb[:, 16 * u : 16 * (u + 1)]))
 
-        y_ps = [psum.tile([P, S], F32, name=f"y_ps{t}") for t in range(PACK)]
+        y_ps = [psum.tile([P, S], F32, tag=f"y_bank{t}", name=f"y_ps{t}") for t in range(PACK)]
         h_ps = [psum.tile([P, S], F32, name=f"h_ps{t}") for t in range(PACK)]
+        last = PACK - 1
+        r_win = [keep.tile([P, 2 * S], F32, tag=f"r_win{t}", name=f"r_win{t}", align_bytes=64) for t in range(PACK)]
         y_win = [keep.tile([P, 2 * S], F32, name=f"y_win{t}", align_bytes=64) for t in range(PACK)]
-        r_win = [keep.tile([P, 2 * S], F32, name=f"r_win{t}", align_bytes=64) for t in range(PACK)]
         h_win = [keep.tile([P, 2 * S], F32, name=f"h_win{t}", align_bytes=64) for t in range(PACK)]
         z = keep.tile([P, PACK, S], F32, name="z", align_bytes=64)
 
-        for t in range(PACK):
+        for t, u in [(0, 0), (1, 0), (0, 1), (1, 1), (2, 0), (2, 1), (3, 0), (3, 1)]:
             cols = slice(t * P, (t + 1) * P)
-            nc.tensor.matmul_mx(out=y_ps[t][:], lhsT=w1_codes[:, cols].bitcast(FP8X4), lhsT_scale=w1_scales[:, cols],
-                                rhs=xw[:].bitcast(FP8X4), rhs_scale=xs[:], start=True, stop=True)
+            places = slice(u * HALF, (u + 1) * HALF)
+            nc.tensor.matmul_mx(out=y_ps[t][:, places], lhsT=w1_codes[:, cols].bitcast(FP8X4), lhsT_scale=w1_scales[:, cols],
+                                rhs=xw[:, places].bitcast(FP8X4), rhs_scale=xs[:, places], start=True, stop=True)
 
+        halves = [slice(0, HALF), slice(HALF, S)]
+        lists_of = [slice(0, HALF // 16), slice(HALF // 16, S // 16)]
+        size = keep.tile([P, PACK, S], F32, name="size", align_bytes=64)
+        root = keep.tile([P, PACK, S], F32, name="root", align_bytes=64)
+        gained = keep.tile([P, PACK, S], F32, name="gained", align_bytes=64)
+        z_grouped = keep.tile([P, PACK * S], BF16, tag="z_grouped", name="z_grouped", align_bytes=64)
+        z_codes = keep.tile([P, S], U32, name="z_codes", align_bytes=64)
+        z_scales = keep.tile([P, S], U8, name="z_scales", align_bytes=64)
+        z_to = z_grouped[:].rearrange("p (u c i t) -> p u c t i", u=2, i=2, t=PACK)
+        z_from = z[:].rearrange("p t (u c i) -> p u c t i", u=2, i=2)
+
+        nc.vector.tensor_copy(y_win[1][:, :S], y_ps[1][:])
+        nc.scalar.activation(size[:, 0, :], y_ps[0][:], ACT.Abs)
         for t in range(PACK):
-            nc.scalar.activation(y_win[t][:, S:], y_ps[t][:], ACT.Abs)
-            nc.scalar.activation(r_win[t][:, S:], y_win[t][:, S:], ACT.Abs_reciprocal_sqrt, bias=half[:])
-            if t < 2:
-                nc.vector.tensor_copy(y_win[t][:, :S], y_ps[t][:])
+            if t != 1:
+                nc.scalar.activation(gained[:, t, :], y_ps[t][:], ACT.Copy, scale=gain[:, t : t + 1])
+            nc.scalar.activation(root[:, t, :], size[:, t, :], ACT.Abs_reciprocal_sqrt, bias=half[:])
+            if t < last:
+                nc.scalar.activation(size[:, t + 1, :], y_ps[t + 1][:], ACT.Abs)
+            if t == 1:
+                nc.vector.scalar_tensor_tensor(r_win[t][:, :S], root[:, t, :], gain[:, t : t + 1], root[:, t, :], MULT, MULT)
+                nc.vector.tensor_tensor(z[:, t, :], r_win[t][:].indirect(n1_sb[:]), y_win[t][:, :S], MULT)
+                continue
+            nc.scalar.activation(r_win[t][:, :S], root[:, t, :], ACT.Square)
+            if t < last:
+                nc.vector.tensor_tensor(z[:, t, :], r_win[t][:].indirect(n1_sb[:]), gained[:, t, :], MULT)
             else:
-                nc.scalar.copy(y_win[t][:, :S], y_ps[t][:])
-            nc.vector.scalar_tensor_tensor(r_win[t][:, :S], r_win[t][:, S:], gain[:, t : t + 1], r_win[t][:, S:], MULT, MULT)
-            nc.vector.tensor_tensor(z[:, t, :], r_win[t][:].indirect(n1_sb[:]), y_win[t][:, :S], MULT)
+                for u in range(2):
+                    nc.vector.tensor_tensor(z[:, t, halves[u]], r_win[t][:].indirect(n1_sb[:, lists_of[u]]), gained[:, t, halves[u]], MULT)
+            if t == 0:
+                nc.vector.tensor_copy(y_win[t][:, :S], y_ps[t][:])
 
+        w2_raw = keep.tile([P, PACK, N], F32, tag="staged", name="w2_raw", align_bytes=64)
+        nc.sync.dma_start(w2_raw[:], w2.rearrange("(p j) c -> p j c", j=PACK))
         w2_grouped = keep.tile([P, PACK * N], BF16, name="w2_grouped", align_bytes=64)
         w2_codes = keep.tile([P, N], U32, name="w2_codes", align_bytes=64)
         w2_scales = keep.tile([P, N], U8, name="w2_scales", align_bytes=64)
-        for m0 in range(0, P, 32):
-            deal(nc.scalar.copy, w2_grouped, w2_raw, m0, m0 + 32)
-
-        z_grouped = keep.tile([P, PACK * S], BF16, name="z_grouped", align_bytes=64)
-        z_codes = keep.tile([P, S], U32, name="z_codes", align_bytes=64)
-        z_scales = keep.tile([P, S], U8, name="z_scales", align_bytes=64)
-        nc.vector.tensor_copy(
-            z_grouped[:].rearrange("p (c i t) -> p c t i", i=2, t=PACK),
-            z[:].rearrange("p t (c i) -> p c t i", i=2),
-        )
+        deal(lambda to, source: nc.gpsimd.tensor_scalar(to, source, 1.0, 0.0, MULT, ADD), w2_grouped, w2_raw, 0, P)
         nc.vector.quantize_mx(out=w2_codes[:].bitcast(FP8X4), scales=w2_scales[:], in_=w2_grouped[:])
-        nc.vector.quantize_mx(out=z_codes[:].bitcast(FP8X4), scales=z_scales[:], in_=z_grouped[:])
 
-        for t in range(PACK):
+        nc.scalar.copy(z_to[:, 0], z_from[:, 0])
+        nc.vector.tensor_copy(z_to[:, 1], z_from[:, 1])
+        for places in halves:
+            nc.vector.quantize_mx(out=z_codes[:, places].bitcast(FP8X4), scales=z_scales[:, places],
+                                  in_=z_grouped[:, PACK * places.start : PACK * places.stop])
+        for t, u in [(0, 0), (1, 0), (0, 1), (1, 1), (2, 0), (2, 1), (3, 0), (3, 1)]:
             cols = slice(t * P, (t + 1) * P)
-            nc.tensor.matmul_mx(out=h_ps[t][:], lhsT=w2_codes[:, cols].bitcast(FP8X4), lhsT_scale=w2_scales[:, cols],
-                                rhs=z_codes[:].bitcast(FP8X4), rhs_scale=z_scales[:], start=True, stop=True)
+            nc.tensor.matmul_mx(out=h_ps[t][:, halves[u]], lhsT=w2_codes[:, cols].bitcast(FP8X4), lhsT_scale=w2_scales[:, cols],
+                                rhs=z_codes[:, halves[u]].bitcast(FP8X4), rhs_scale=z_scales[:, halves[u]], start=True, stop=True)
 
-        y3_first = keep.tile([P, S], F32, name="y3_first")
-        nc.vector.tensor_copy(y3_first[:], y_win[0][:].indirect(n3_sb[:]))
+        nc.scalar.copy(y_win[2][:, :S], y_ps[2][:])
+        y3 = [keep.tile([P, S], F32, name=f"y3_{t}") for t in range(2)]
+        y3.append(keep.tile([P, S], F32, tag="z_grouped", name="y3_2", align_bytes=64))
+        for t in (1, 0, 2):
+            nc.vector.tensor_copy(y3[t][:], y_win[t][:].indirect(n3_sb[:]))
 
         out_rows = out.rearrange("(p t) j -> p t j", t=PACK)
+        first = [keep.tile([P, S], F32, name=f"first{t}") for t in range(PACK)]
+        second = [keep.tile([P, S], F32, name=f"second{t}") for t in range(PACK)]
+        result = [keep.tile([P, S], F32, name=f"result{t}") for t in range(PACK)]
+
+        def finish(t, places, op):
+            nc.vector.tensor_tensor(result[t][:, places], second[t][:, places], first[t][:, places], op)
+            nc.sync.dma_start(out_rows[:, t, places], result[t][:, places])
+
+        def finish_by_transposes(t, u):
+            turned_ps = psum.tile([P, HALF], F32, tag=f"y_bank{u}", name=f"turned_ps{t}{u}")
+            back_ps = psum.tile([P, HALF], F32, tag=f"y_bank{2 + u}", name=f"back_ps{t}{u}")
+            turned = keep.tile([P, HALF], F32, name=f"turned{t}{u}")
+            for c in range(0, HALF, P):
+                block = slice(u * HALF + c, u * HALF + c + P)
+                nc.tensor.matmul(turned_ps[:, c : c + P], first[t][:, block], identity[:], is_transpose=True, start=True, stop=False)
+                nc.tensor.matmul(turned_ps[:, c : c + P], second[t][:, block], identity[:], is_transpose=True, start=False, stop=True)
+            nc.scalar.copy(turned[:], turned_ps[:])
+            for c in range(0, HALF, P):
+                nc.tensor.transpose(back_ps[:, c : c + P], turned[:, c : c + P], identity[:])
+            nc.scalar.copy(result[t][:, halves[u]], back_ps[:])
+            nc.scalar.dma_start(out_rows[:, t, halves[u]], result[t][:, halves[u]])
+
         for t in range(PACK):
-            nc.scalar.activation(h_win[t][:, :S], h_ps[t][:], ACT.Copy, scale=0.75)
-            if t == 0:
-                nc.vector.tensor_tensor(h_win[t][:, S:], y3_first[:], h_win[t][:, :S], MULT)
-            else:
-                nc.vector.tensor_tensor(h_win[t][:, S:], y_win[t][:].indirect(n3_sb[:]), h_win[t][:, :S], MULT)
-            second = keep.tile([P, S], F32, name=f"second{t}")
-            nc.vector.tensor_tensor(second[:], h_win[t][:].indirect(n2_sb[:]), y_win[t][:, :S], MULT)
-            result = keep.tile([P, S], F32, name=f"result{t}")
-            nc.vector.tensor_tensor(result[:], h_win[t][:, S:], second[:], SUB)
-            nc.sync.dma_start(out_rows[:, t, :], result[:])
+            nc.scalar.activation(h_win[t][:, :S], h_ps[t][:], ACT.Copy, scale=-0.75)
+            if t == 1:
+                nc.scalar.copy(y_win[last][:, :S], y_ps[last][:])
+        for t in range(last):
+            nc.vector.scalar_tensor_tensor(first[t][:], h_ps[t][:], 0.75, y3[t][:], MULT, MULT)
+            for u in range(2):
+                nc.vector.tensor_tensor(second[t][:, halves[u]], h_win[t][:].indirect(n2_sb[:, lists_of[u]]), y_win[t][:, halves[u]], MULT)
+                finish_by_transposes(t, u)
+        nc.vector.tensor_tensor(first[last][:], y_win[last][:].indirect(n3_sb[:]), h_win[last][:, :S], MULT)
+        for u in range(2):
+            nc.vector.tensor_tensor(second[last][:, halves[u]], h_win[last][:].indirect(n2_sb[:, lists_of[u]]), y_win[last][:, halves[u]], MULT)
+        for u in range(2):
+            finish(last, halves[u], SUB)

@@ -34,11 +34,11 @@ def tile_picked_skipcrossbnorm_none_p_kernel(tc, x_words, x_scales, w1, gn, w2, 
         n2_sb = lists.tile([P, S // 16], U16, name="n2_sb")
         n3_sb = lists.tile([P, S // 16], U16, name="n3_sb")
 
-        xs_all = keep.tile([P, T], U8, tag="staged", name="xs_all", align_bytes=64)
+        xs_all = keep.tile([P, T], U8, name="xs_all", align_bytes=64)
         xw_all = keep.tile([P, T], I32, name="xw_all", align_bytes=64)
         w1_raw = keep.tile([P, PACK, H], F32, name="w1_raw", align_bytes=64)
         gain = keep.tile([P, PACK], F32, name="gain")
-        four = keep.tile([P, 1], F32, name="four")
+        four = keep.tile([P, 1], F32, tag="staged", name="four", align_bytes=64)
         half = keep.tile([P, 1], F32, name="half")
 
         nc.gpsimd.memset(xs_all[:].bitcast(I32), 0)
@@ -58,10 +58,10 @@ def tile_picked_skipcrossbnorm_none_p_kernel(tc, x_words, x_scales, w1, gn, w2, 
         nc.sync.dma_start(n2_sb[:], n2)
         nc.sync.dma_start(xw_all[:], x_words[0].rearrange("p n t -> p (n t)").bitcast(I32))
 
-        def deal(engine_copy, grouped, raw, m0, m1):
-            engine_copy(
-                grouped[:].rearrange("p (t m j) -> p m t j", t=PACK, j=PACK)[:, m0:m1],
-                raw[:].rearrange("p j (m t) -> p m t j", t=PACK)[:, m0:m1],
+        def dealt_views(grouped, raw):
+            return (
+                grouped[:].rearrange("p (t m j) -> p m t j", t=PACK, j=PACK),
+                raw[:].rearrange("p j (m t) -> p m t j", t=PACK),
             )
 
         xs = keep.tile([P, S], U8, name="xs", align_bytes=64)
@@ -70,8 +70,9 @@ def tile_picked_skipcrossbnorm_none_p_kernel(tc, x_words, x_scales, w1, gn, w2, 
         w1_codes = keep.tile([P, H], U32, name="w1_codes", align_bytes=64)
         w1_scales = keep.tile([P, H], U8, name="w1_scales", align_bytes=64)
         nc.vector.tensor_copy(xs[:], xs_all[:].indirect(offs_sb[:]))
-        deal(nc.scalar.copy, w1_grouped, w1_raw, 0, 64)
-        deal(nc.vector.tensor_copy, w1_grouped, w1_raw, 64, 128)
+        w1_to, w1_from = dealt_views(w1_grouped, w1_raw)
+        nc.scalar.copy(w1_to[:, :72], w1_from[:, :72])
+        nc.vector.tensor_copy(w1_to[:, 72:], w1_from[:, 72:])
         nc.vector.quantize_mx(out=w1_codes[:].bitcast(FP8X4), scales=w1_scales[:], in_=w1_grouped[:])
         HALF = S // 2
         for u in range(2):
@@ -81,7 +82,7 @@ def tile_picked_skipcrossbnorm_none_p_kernel(tc, x_words, x_scales, w1, gn, w2, 
         h_ps = [psum.tile([P, S], F32, name=f"h_ps{t}") for t in range(PACK)]
         last = PACK - 1
         r_win = [keep.tile([P, 2 * S], F32, tag=f"r_win{t}", name=f"r_win{t}", align_bytes=64) for t in range(PACK)]
-        y_win = [keep.tile([P, 2 * S], F32, name=f"y_win{t}", align_bytes=64) for t in range(PACK)]
+        y_win = [keep.tile([P, 2 * S], F32, name=f"y_win{t}", align_bytes=64) for t in range(2)]
         h_win = [keep.tile([P, 2 * S], F32, name=f"h_win{t}", align_bytes=64) for t in range(PACK)]
         z = keep.tile([P, PACK, S], F32, name="z", align_bytes=64)
 
@@ -94,8 +95,8 @@ def tile_picked_skipcrossbnorm_none_p_kernel(tc, x_words, x_scales, w1, gn, w2, 
         halves = [slice(0, HALF), slice(HALF, S)]
         lists_of = [slice(0, HALF // 16), slice(HALF // 16, S // 16)]
         size = keep.tile([P, PACK, S], F32, name="size", align_bytes=64)
-        root = keep.tile([P, PACK, S], F32, name="root", align_bytes=64)
-        gained = keep.tile([P, PACK, S], F32, name="gained", align_bytes=64)
+        root = keep.tile([P, PACK, S], F32, tag="root", name="root", align_bytes=64)
+        gained = keep.tile([P, PACK, S], F32, tag="gained", name="gained", align_bytes=64)
         z_grouped = keep.tile([P, PACK * S], BF16, tag="z_grouped", name="z_grouped", align_bytes=64)
         z_codes = keep.tile([P, S], U32, name="z_codes", align_bytes=64)
         z_scales = keep.tile([P, S], U8, name="z_scales", align_bytes=64)
@@ -128,7 +129,8 @@ def tile_picked_skipcrossbnorm_none_p_kernel(tc, x_words, x_scales, w1, gn, w2, 
         w2_grouped = keep.tile([P, PACK * N], BF16, name="w2_grouped", align_bytes=64)
         w2_codes = keep.tile([P, N], U32, name="w2_codes", align_bytes=64)
         w2_scales = keep.tile([P, N], U8, name="w2_scales", align_bytes=64)
-        deal(lambda to, source: nc.gpsimd.tensor_scalar(to, source, 1.0, 0.0, MULT, ADD), w2_grouped, w2_raw, 0, P)
+        w2_to, w2_from = dealt_views(w2_grouped, w2_raw)
+        nc.gpsimd.tensor_scalar(w2_to, w2_from, 1.0, 0.0, MULT, ADD)
         nc.vector.quantize_mx(out=w2_codes[:].bitcast(FP8X4), scales=w2_scales[:], in_=w2_grouped[:])
 
         nc.scalar.copy(z_to[:, 0], z_from[:, 0])
@@ -141,7 +143,10 @@ def tile_picked_skipcrossbnorm_none_p_kernel(tc, x_words, x_scales, w1, gn, w2, 
             nc.tensor.matmul_mx(out=h_ps[t][:, halves[u]], lhsT=w2_codes[:, cols].bitcast(FP8X4), lhsT_scale=w2_scales[:, cols],
                                 rhs=z_codes[:, halves[u]].bitcast(FP8X4), rhs_scale=z_scales[:, halves[u]], start=True, stop=True)
 
-        nc.scalar.copy(y_win[2][:, :S], y_ps[2][:])
+        y_win.append(keep.tile([P, 2 * S], F32, tag="root", name="y_win2", align_bytes=64))
+        y_win.append(keep.tile([P, 2 * S], F32, tag="gained", name="y_win3", align_bytes=64))
+        for t in (2, 3):
+            nc.scalar.copy(y_win[t][:, :S], y_ps[t][:])
         y3 = [keep.tile([P, S], F32, name=f"y3_{t}") for t in range(2)]
         y3.append(keep.tile([P, S], F32, tag="z_grouped", name="y3_2", align_bytes=64))
         for t in (1, 0, 2):
@@ -152,8 +157,8 @@ def tile_picked_skipcrossbnorm_none_p_kernel(tc, x_words, x_scales, w1, gn, w2, 
         second = [keep.tile([P, S], F32, name=f"second{t}") for t in range(PACK)]
         result = [keep.tile([P, S], F32, name=f"result{t}") for t in range(PACK)]
 
-        def finish(t, places, op):
-            nc.vector.tensor_tensor(result[t][:, places], second[t][:, places], first[t][:, places], op)
+        def finish(t, places):
+            nc.vector.tensor_tensor(result[t][:, places], second[t][:, places], first[t][:, places], SUB)
             nc.sync.dma_start(out_rows[:, t, places], result[t][:, places])
 
         def finish_by_transposes(t, u):
@@ -172,8 +177,6 @@ def tile_picked_skipcrossbnorm_none_p_kernel(tc, x_words, x_scales, w1, gn, w2, 
 
         for t in range(PACK):
             nc.scalar.activation(h_win[t][:, :S], h_ps[t][:], ACT.Copy, scale=-0.75)
-            if t == 1:
-                nc.scalar.copy(y_win[last][:, :S], y_ps[last][:])
         for t in range(last):
             nc.vector.scalar_tensor_tensor(first[t][:], h_ps[t][:], 0.75, y3[t][:], MULT, MULT)
             for u in range(2):
@@ -183,4 +186,4 @@ def tile_picked_skipcrossbnorm_none_p_kernel(tc, x_words, x_scales, w1, gn, w2, 
         for u in range(2):
             nc.vector.tensor_tensor(second[last][:, halves[u]], h_win[last][:].indirect(n2_sb[:, lists_of[u]]), y_win[last][:, halves[u]], MULT)
         for u in range(2):
-            finish(last, halves[u], SUB)
+            finish(last, halves[u])

@@ -157,8 +157,8 @@ def tile_picked_skipcrossbnorm_none_p_kernel(tc, x_words, x_scales, w1, gn, w2, 
         second = [keep.tile([P, S], F32, name=f"second{t}") for t in range(PACK)]
         result = [keep.tile([P, S], F32, name=f"result{t}") for t in range(PACK)]
 
-        def finish(t, places):
-            nc.vector.tensor_tensor(result[t][:, places], second[t][:, places], first[t][:, places], SUB)
+        def finish(t, places, op):
+            nc.vector.tensor_tensor(result[t][:, places], second[t][:, places], first[t][:, places], op)
             nc.sync.dma_start(out_rows[:, t, places], result[t][:, places])
 
         def finish_by_transposes(t, u):
@@ -181,9 +181,11 @@ def tile_picked_skipcrossbnorm_none_p_kernel(tc, x_words, x_scales, w1, gn, w2, 
             nc.vector.scalar_tensor_tensor(first[t][:], h_ps[t][:], 0.75, y3[t][:], MULT, MULT)
             for u in range(2):
                 nc.vector.tensor_tensor(second[t][:, halves[u]], h_win[t][:].indirect(n2_sb[:, lists_of[u]]), y_win[t][:, halves[u]], MULT)
-                finish_by_transposes(t, u)
+                if (t, u) != (2, 1):
+                    finish_by_transposes(t, u)
         nc.vector.tensor_tensor(first[last][:], y_win[last][:].indirect(n3_sb[:]), h_win[last][:, :S], MULT)
+        finish(2, halves[1], ADD)
         for u in range(2):
             nc.vector.tensor_tensor(second[last][:, halves[u]], h_win[last][:].indirect(n2_sb[:, lists_of[u]]), y_win[last][:, halves[u]], MULT)
         for u in range(2):
-            finish(last, halves[u])
+            finish(last, halves[u], SUB)

from contextlib import ExitStack

import concourse.mybir as mybir
from concourse.masks import make_identity

K, T, S, N, H = 512, 2048, 512, 512, 512
FLOPS = 2 * K * H * S + 2 * H * N * S

F32 = mybir.dt.float32
BF16 = mybir.dt.bfloat16
I32 = mybir.dt.int32
U32 = mybir.dt.uint32
U16 = mybir.dt.uint16
U8 = mybir.dt.uint8
FP8X4 = mybir.dt.float8_e4m3fn_x4
ACT = mybir.ActivationFunctionType
MULT = mybir.AluOpType.mult
ADD = mybir.AluOpType.add
SUB = mybir.AluOpType.subtract

P = 128
PACK = 4


def tile_picked_skipcrossbnorm_none_p_kernel(tc, x_words, x_scales, w1, gn, w2, offs, n1, n2, n3, out):
    nc = tc.nc
    with ExitStack() as ctx:
        lists = ctx.enter_context(tc.tile_pool(name="lists", bufs=1))
        keep = ctx.enter_context(tc.tile_pool(name="keep", bufs=1))
        psum = ctx.enter_context(tc.psum_pool(name="psum", bufs=1))

        offs_sb = lists.tile([P, S // 16], U16, name="offs_sb")
        n1_sb = lists.tile([P, S // 16], U16, name="n1_sb")
        n2_sb = lists.tile([P, S // 16], U16, name="n2_sb")
        n3_sb = lists.tile([P, S // 16], U16, name="n3_sb")

        xs_all = keep.tile([P, T], U8, name="xs_all", align_bytes=64)
        xw_all = keep.tile([P, T], I32, name="xw_all", align_bytes=64)
        w1_raw = keep.tile([P, PACK, H], F32, name="w1_raw", align_bytes=64)
        gain = keep.tile([P, PACK], F32, name="gain")
        four = keep.tile([P, 1], F32, tag="staged", name="four", align_bytes=64)
        half = keep.tile([P, 1], F32, name="half")

        nc.gpsimd.memset(xs_all[:].bitcast(I32), 0)
        nc.gpsimd.memset(four[:], 4.0)
        for q in range(4):
            nc.scalar.dma_start(xs_all[32 * q : 32 * q + 4, :].bitcast(I32), x_scales[0, 4 * q : 4 * q + 4, :].bitcast(I32))
        nc.scalar.activation(half[:], four[:], ACT.Abs_reciprocal_sqrt)

        nc.gpsimd.dma_start(gain[:], gn.rearrange("(p t) o -> p (t o)", t=PACK))
        identity = keep.tile([P, P], F32, name="identity")
        make_identity(nc, identity[:])

        nc.sync.dma_start(offs_sb[:], offs)
        nc.sync.dma_start(n1_sb[:], n1)
        nc.sync.dma_start(w1_raw[:], w1.rearrange("(p j) c -> p j c", j=PACK))
        nc.sync.dma_start(n3_sb[:], n3)
        nc.sync.dma_start(n2_sb[:], n2)
        nc.sync.dma_start(xw_all[:], x_words[0].rearrange("p n t -> p (n t)").bitcast(I32))

        def dealt_views(grouped, raw):
            return (
                grouped[:].rearrange("p (t m j) -> p m t j", t=PACK, j=PACK),
                raw[:].rearrange("p j (m t) -> p m t j", t=PACK),
            )

        xs = keep.tile([P, S], U8, name="xs", align_bytes=64)
        xw = keep.tile([P, S], U32, name="xw", align_bytes=64)
        w1_grouped = keep.tile([P, PACK * H], BF16, name="w1_grouped", align_bytes=64)
        w1_codes = keep.tile([P, H], U32, name="w1_codes", align_bytes=64)
        w1_scales = keep.tile([P, H], U8, name="w1_scales", align_bytes=64)
        nc.vector.tensor_copy(xs[:], xs_all[:].indirect(offs_sb[:]))
        w1_to, w1_from = dealt_views(w1_grouped, w1_raw)
        nc.scalar.copy(w1_to[:, :72], w1_from[:, :72])
        nc.vector.tensor_copy(w1_to[:, 72:], w1_from[:, 72:])
        nc.vector.quantize_mx(out=w1_codes[:].bitcast(FP8X4), scales=w1_scales[:], in_=w1_grouped[:])
        HALF = S // 2
        for u in range(2):
            nc.vector.tensor_copy(xw[:, u * HALF : (u + 1) * HALF], xw_all[:].bitcast(U32).indirect(offs_sb[:, 16 * u : 16 * (u + 1)]))

        y_ps = [psum.tile([P, S], F32, tag=f"y_bank{t}", name=f"y_ps{t}") for t in range(PACK)]
        h_ps = [psum.tile([P, S], F32, name=f"h_ps{t}") for t in range(PACK)]
        last = PACK - 1
        r_win = [keep.tile([P, 2 * S], F32, tag=f"r_win{t}", name=f"r_win{t}", align_bytes=64) for t in range(PACK)]
        y_win = [keep.tile([P, 2 * S], F32, name=f"y_win{t}", align_bytes=64) for t in range(2)]
        h_win = [keep.tile([P, 2 * S], F32, name=f"h_win{t}", align_bytes=64) for t in range(PACK)]
        z = keep.tile([P, PACK, S], F32, name="z", align_bytes=64)

        for t, u in [(0, 0), (1, 0), (0, 1), (1, 1), (2, 0), (2, 1), (3, 0), (3, 1)]:
            cols = slice(t * P, (t + 1) * P)
            places = slice(u * HALF, (u + 1) * HALF)
            nc.tensor.matmul_mx(out=y_ps[t][:, places], lhsT=w1_codes[:, cols].bitcast(FP8X4), lhsT_scale=w1_scales[:, cols],
                                rhs=xw[:, places].bitcast(FP8X4), rhs_scale=xs[:, places], start=True, stop=True)

        halves = [slice(0, HALF), slice(HALF, S)]
        lists_of = [slice(0, HALF // 16), slice(HALF // 16, S // 16)]
        size = keep.tile([P, PACK, S], F32, name="size", align_bytes=64)
        root = keep.tile([P, PACK, S], F32, tag="root", name="root", align_bytes=64)
        gained = keep.tile([P, PACK, S], F32, tag="gained", name="gained", align_bytes=64)
        z_grouped = keep.tile([P, PACK * S], BF16, tag="z_grouped", name="z_grouped", align_bytes=64)
        z_codes = keep.tile([P, S], U32, name="z_codes", align_bytes=64)
        z_scales = keep.tile([P, S], U8, name="z_scales", align_bytes=64)
        z_to = z_grouped[:].rearrange("p (u c i t) -> p u c t i", u=2, i=2, t=PACK)
        z_from = z[:].rearrange("p t (u c i) -> p u c t i", u=2, i=2)

        nc.vector.tensor_copy(y_win[1][:, :S], y_ps[1][:])
        nc.scalar.activation(size[:, 0, :], y_ps[0][:], ACT.Abs)
        for t in range(PACK):
            if t != 1:
                nc.scalar.activation(gained[:, t, :], y_ps[t][:], ACT.Copy, scale=gain[:, t : t + 1])
            nc.scalar.activation(root[:, t, :], size[:, t, :], ACT.Abs_reciprocal_sqrt, bias=half[:])
            if t < last:
                nc.scalar.activation(size[:, t + 1, :], y_ps[t + 1][:], ACT.Abs)
            if t == 1:
                nc.vector.scalar_tensor_tensor(r_win[t][:, :S], root[:, t, :], gain[:, t : t + 1], root[:, t, :], MULT, MULT)
                nc.vector.tensor_tensor(z[:, t, :], r_win[t][:].indirect(n1_sb[:]), y_win[t][:, :S], MULT)
                continue
            nc.scalar.activation(r_win[t][:, :S], root[:, t, :], ACT.Square)
            if t < last:
                nc.vector.tensor_tensor(z[:, t, :], r_win[t][:].indirect(n1_sb[:]), gained[:, t, :], MULT)
            else:
                for u in range(2):
                    nc.vector.tensor_tensor(z[:, t, halves[u]], r_win[t][:].indirect(n1_sb[:, lists_of[u]]), gained[:, t, halves[u]], MULT)
            if t == 0:
                nc.vector.tensor_copy(y_win[t][:, :S], y_ps[t][:])

        w2_raw = keep.tile([P, PACK, N], F32, tag="staged", name="w2_raw", align_bytes=64)
        nc.sync.dma_start(w2_raw[:], w2.rearrange("(p j) c -> p j c", j=PACK))
        w2_grouped = keep.tile([P, PACK * N], BF16, name="w2_grouped", align_bytes=64)
        w2_codes = keep.tile([P, N], U32, name="w2_codes", align_bytes=64)
        w2_scales = keep.tile([P, N], U8, name="w2_scales", align_bytes=64)
        w2_to, w2_from = dealt_views(w2_grouped, w2_raw)
        nc.gpsimd.tensor_scalar(w2_to, w2_from, 1.0, 0.0, MULT, ADD)
        nc.vector.quantize_mx(out=w2_codes[:].bitcast(FP8X4), scales=w2_scales[:], in_=w2_grouped[:])

        nc.scalar.copy(z_to[:, 0], z_from[:, 0])
        nc.vector.tensor_copy(z_to[:, 1], z_from[:, 1])
        for places in halves:
            nc.vector.quantize_mx(out=z_codes[:, places].bitcast(FP8X4), scales=z_scales[:, places],
                                  in_=z_grouped[:, PACK * places.start : PACK * places.stop])
        for t, u in [(0, 0), (1, 0), (0, 1), (1, 1), (2, 0), (2, 1), (3, 0), (3, 1)]:
            cols = slice(t * P, (t + 1) * P)
            nc.tensor.matmul_mx(out=h_ps[t][:, halves[u]], lhsT=w2_codes[:, cols].bitcast(FP8X4), lhsT_scale=w2_scales[:, cols],
                                rhs=z_codes[:, halves[u]].bitcast(FP8X4), rhs_scale=z_scales[:, halves[u]], start=True, stop=True)

        y_win.append(keep.tile([P, 2 * S], F32, tag="root", name="y_win2", align_bytes=64))
        y_win.append(keep.tile([P, 2 * S], F32, tag="gained", name="y_win3", align_bytes=64))
        for t in (2, 3):
            nc.scalar.copy(y_win[t][:, :S], y_ps[t][:])
        y3 = [keep.tile([P, S], F32, name=f"y3_{t}") for t in range(2)]
        y3.append(keep.tile([P, S], F32, tag="z_grouped", name="y3_2", align_bytes=64))
        for t in (1, 0, 2):
            nc.vector.tensor_copy(y3[t][:], y_win[t][:].indirect(n3_sb[:]))

        out_rows = out.rearrange("(p t) j -> p t j", t=PACK)
        first = [keep.tile([P, S], F32, name=f"first{t}") for t in range(PACK)]
        second = [keep.tile([P, S], F32, name=f"second{t}") for t in range(PACK)]
        result = [keep.tile([P, S], F32, name=f"result{t}") for t in range(PACK)]

        def finish(t, places, op):
            nc.vector.tensor_tensor(result[t][:, places], second[t][:, places], first[t][:, places], op)
            nc.sync.dma_start(out_rows[:, t, places], result[t][:, places])

        def finish_by_transposes(t, u):
            turned_ps = psum.tile([P, HALF], F32, tag=f"y_bank{u}", name=f"turned_ps{t}{u}")
            back_ps = psum.tile([P, HALF], F32, tag=f"y_bank{2 + u}", name=f"back_ps{t}{u}")
            turned = keep.tile([P, HALF], F32, name=f"turned{t}{u}")
            for c in range(0, HALF, P):
                block = slice(u * HALF + c, u * HALF + c + P)
                nc.tensor.matmul(turned_ps[:, c : c + P], first[t][:, block], identity[:], is_transpose=True, start=True, stop=False)
                nc.tensor.matmul(turned_ps[:, c : c + P], second[t][:, block], identity[:], is_transpose=True, start=False, stop=True)
            nc.scalar.copy(turned[:], turned_ps[:])
            for c in range(0, HALF, P):
                nc.tensor.transpose(back_ps[:, c : c + P], turned[:, c : c + P], identity[:])
            nc.scalar.copy(result[t][:, halves[u]], back_ps[:])
            nc.scalar.dma_start(out_rows[:, t, halves[u]], result[t][:, halves[u]])

        for t in range(PACK):
            nc.scalar.activation(h_win[t][:, :S], h_ps[t][:], ACT.Copy, scale=-0.75)
        for t in range(last):
            nc.vector.scalar_tensor_tensor(first[t][:], h_ps[t][:], 0.75, y3[t][:], MULT, MULT)
            for u in range(2):
                nc.vector.tensor_tensor(second[t][:, halves[u]], h_win[t][:].indirect(n2_sb[:, lists_of[u]]), y_win[t][:, halves[u]], MULT)
                if (t, u) != (2, 1):
                    finish_by_transposes(t, u)
        nc.vector.tensor_tensor(first[last][:], y_win[last][:].indirect(n3_sb[:]), h_win[last][:, :S], MULT)
        finish(2, halves[1], ADD)
        for u in range(2):
            nc.vector.tensor_tensor(second[last][:, halves[u]], h_win[last][:].indirect(n2_sb[:, lists_of[u]]), y_win[last][:, halves[u]], MULT)
        for u in range(2):
            finish(last, halves[u], SUB)
